import numpy as np, ml_dtypes
CORES = [23,119,17,113]
N = 4
BF = ml_dtypes.bfloat16
def f(rng, *shape):
    return (rng.standard_normal(shape, dtype=np.float32) * np.exp2(rng.integers(-2, 3, shape[:-1] + (1,)))).astype(BF)
def wide(rng, *shape):
    v = f(rng, *shape).astype(np.float32); k = shape[:-2] + (1, shape[-1])
    return (v * np.exp2(rng.integers(-6, 7, k)) * (rng.random(k) > 0.0625)).astype(BF)
def gentries(a):
    return np.ascontiguousarray(a.reshape(8, 16, -1).transpose(0, 2, 1)).reshape(8, -1)
def gtable(e):
    e = np.asarray(e); return np.ascontiguousarray(e.reshape(8, -1, 16).transpose(0, 2, 1)).reshape(128, -1).astype(np.int32)
E, S, D, F, R, V = 2048, 256, 64, 4, 3, 16384
W = E + (N - 1) * S
def arrive(a, snd):
    out = []
    for r in range(N):
        part = [a[r]]
        for t in range(1, N):
            q = (r + t) % N; p = gentries(snd[q]).reshape(8, N - 1, S)[:, N - 1 - t]
            part.append(np.take_along_axis(a[q], p[:, None, :], axis=2))
        out.append(np.concatenate(part, axis=2))
    return np.stack(out)
def slots(rng, lo, hi):
    return np.stack([rng.permuted(np.tile(np.arange(lo, hi), (8 * (N - 1), 1)), axis=1)[:, :S].reshape(8, N - 1, S) for r in range(N)])
def preds(rng):
    v = np.where(rng.random((N, 8, F, E)) < 0.5, rng.integers(0, E, (N, 8, F, E)), rng.integers(E, W, (N, 8, F, E)))
    v[:, :, 1] = np.where(rng.random((N, 8, E)) < 0.0625, v[:, :, 0], v[:, :, 1]); return v
def nodes(rng):
    return rng.integers(0, V, (N, 8, E))
def codes(rng):
    return rng.integers(0, D, (N, 8, E))
def make(rng, v, p, s, c):
    snd = np.stack([gtable(p[r].reshape(8, -1)) for r in range(N)]); a = arrive(s[:, :, None, :], snd)
    sf = np.take_along_axis(a, v.reshape(N, 8, 1, F * E), axis=3).reshape(N, 8, F, E)
    d = np.take_along_axis(sf, rng.integers(0, F, (N, 8, 1, E)), axis=2)[:, :, 0]; u = rng.integers(0, 8, (N, 8, E))
    d = np.where(u < 5, d, np.where(u < 7, d ^ 1, rng.integers(0, V, (N, 8, E))))
    return {"x": f(rng, N, 128, E), "tab": (rng.random((N, 128, D * D), dtype=np.float32) * 2 - 1).astype(BF), "dirs": c.astype(np.int32), "srcs": s.astype(np.int32), "dsts": d.astype(np.int32),
            "nb": np.stack([gtable(v[r].reshape(8, -1)) for r in range(N)]), "snd": snd}
def setup_inputs(rng):
    return make(rng, preds(rng), slots(rng, 0, E), nodes(rng), codes(rng))
def setup_inputs_ends(rng):
    p = slots(rng, 1, E - 1); p[..., 0] = E - 1; p[..., S - 1] = 0
    v = np.where(rng.random((N, 8, F, E)) < 0.75, rng.choice(np.array([0, 1, E - 1, E, E + S - 1, E + S, W - S, W - 1]), (N, 8, F, E)), preds(rng))
    return make(rng, v, p, rng.choice(np.array([0, 1, V - 2, V - 1]), (N, 8, E)), rng.choice(np.array([0, 1, D - 2, D - 1]), (N, 8, E)))
def setup_inputs_back(rng):
    s = 2 * rng.integers(0, V // 2, (1, 8, 1)) + rng.integers(0, 2, (N, 8, E))
    return make(rng, preds(rng), slots(rng, 0, E), s, codes(rng))
def setup_inputs_far(rng):
    v = rng.integers(E, W, (N, 8, F, E)); a = rng.permutation(N); t = int(rng.integers(0, N - 1))
    v[a[0]] = E + t * S + rng.integers(0, S, (8, F, E)); v[a[1]] = rng.integers(0, E, (8, F, E))
    p = slots(rng, 0, E); p[:] = p[:, :, :1].copy()
    return make(rng, v, p, nodes(rng), codes(rng))
def setup_inputs_alike(rng):
    v = preds(rng); v[:] = v[:, :, :1].copy()
    c = np.broadcast_to(rng.integers(0, D, (N, 8, 1)), (N, 8, E))
    return make(rng, v, slots(rng, 0, E), nodes(rng), c)
def setup_inputs_spread(rng):
    d = setup_inputs(rng); d["x"] = wide(rng, N, 128, E); return d
def check_inputs(d):
    bad = []
    for name, top in (("nb", W), ("snd", E), ("dirs", D), ("srcs", V), ("dsts", V)):
        if not ((d[name] >= 0) & (d[name] < top)).all(): bad.append(name + " in its range")
    p = np.stack([gentries(d["snd"][r]).reshape(8 * (N - 1), S) for r in range(N)])
    if not (np.diff(np.sort(p, axis=2), axis=2) > 0).all(): bad.append("different edges in the slots of a pair and group")
    if not (np.abs(d["x"].astype(np.float64)) <= 2.0 ** 40).all(): bad.append("x finite and at most 2**40 in size")
    if not (np.abs(d["tab"].astype(np.float64)) <= 1).all(): bad.append("tab at most 1 in size")
    return bad
def reference(x, tab, dirs, srcs, dsts, nb, snd):
    xs = x.astype(np.float64).reshape(N, 8, 16, E); v = np.stack([gentries(nb[r]) for r in range(N)])
    df = np.take_along_axis(arrive(dirs[:, :, None, :], snd)[:, :, 0], v, axis=2)
    sf = np.take_along_axis(arrive(srcs[:, :, None, :], snd)[:, :, 0], v, axis=2)
    off = D * df + np.tile(dirs, (1, 1, F)); back = sf == np.tile(dsts, (1, 1, F))
    w = []
    for r in range(N):
        c = np.take_along_axis(tab[r].astype(np.float64).reshape(8, 16, D * D), off[r][:, None, :], axis=2)
        w.append(np.where(back[r][:, None, :], 0.0, c * 0.25))
    m = xs
    for k in range(R):
        a = arrive(m, snd); new = []
        for r in range(N):
            term = w[r] * np.take_along_axis(a[r], v[r][:, None, :], axis=2)
            new.append(np.maximum(xs[r] + np.sum(term.reshape(8, 16, F, E), axis=2), 0.0))
        m = np.stack(new)
    return {"y": m.reshape(N, 128, E).astype(np.float32)}

from concourse.bass import DstId, RemoteDMATransfer
from concourse.mybir import AluOpType, ActivationFunctionType

E, S, NR, F = 2048, 256, 4, 4
W = E + (NR - 1) * S
Q = 512
TO = 16

SCRATCH = {
    "raw": ("sbuf", [128, 384], "int32"),
    "cmp": ("sbuf", [128, 640], "bfloat16"),
    "KW": ("sbuf", [128, W], "bfloat16"),
    "XW": ("sbuf", [128, W], "bfloat16"),
    "DR": ("sbuf", [128, E], "bfloat16"),
    "MW1": ("sbuf", [128, W], "float32"),
    "MW2": ("sbuf", [128, W], "float32"),
    "YB": ("sbuf", [128, E], "float32"),
    "TAB": ("sbuf", [128, TO + 4096], "bfloat16"),
    "G": ("sbuf", [128, F * E], "bfloat16"),
    "WT": ("sbuf", [128, F * E], "float32"),
    "TM": ("sbuf", [128, F * E], "float32"),
    "XG": ("sbuf", [128, F * E], "float32"),
    "sndr": ("sbuf", [128, 48], "int32"),
    "sndu": ("sbuf", [128, 48], "uint16"),
    "nbr": ("sbuf", [128, 512], "int32"),
    "nbu": ("sbuf", [128, 512], "uint16"),
    "offu": ("sbuf", [128, 512], "uint16"),
    "zi": ("sbuf", [128, 512], "int32"),
    "ai": ("sbuf", [128, 512], "int32"),
    "sq": ("sbuf", [128, 512], "float32"),
    "ND": ("sbuf", [128, 128], "float32"),
    "pv": ("sbuf", [128, 128], "float32"),
    "I32": ("sbuf", [128, 128], "float32"),
    "Ibf": ("sbuf", [128, 128], "bfloat16"),
    "base": ("sbuf", [128, 432], "bfloat16"),
    "tiny": ("sbuf", [128, 64], "float32"),
    "SK": ("sbuf", [128, 768], "bfloat16"),
    "SX": ("sbuf", [128, 768], "bfloat16"),
    "SM1": ("sbuf", [128, 768], "float32"),
    "SM2": ("sbuf", [128, 768], "float32"),
}
for _i in range(4):
    SCRATCH["PA%d" % _i] = ("psum", [128, Q], "float32")
    SCRATCH["PB%d" % _i] = ("psum", [128, Q], "float32")

SEMAPHORES = ["cv", "ca", "cp", "cg", "sent", "arrX", "arrK", "arr1", "arr2",
              "l_ds", "l_dd", "l_snd", "l_x", "l_nb", "l_tab", "l_kw", "l_dr", "st"]

CFG = {
    "pe": {1: [4, 4, 3, 3], 2: [3, 3, 3, 3], 3: [3, 3, 3, 3]},
    "v_list": "x00 x01 k00 k01 k10 k11",
    "a_list": "x02 x03 k02 k03 k12 k13 k20 k21 k22 k23 x10 x11 x12 x13 k30 k31 k32 k33 x20 x21 x22 x23 x30 x31 x32 x33",
    "ipos": [0, 0, 2],
    "wpos": [(0, 0), (0, 2), (1, 3)],
    "w_v": 4,
    "order": {2: "t0 t1 t2 t3 m0 m1 f0 m2 f1 m3 f2 f3", 3: "t0 t1 m0 t2 f0 m1 t3 f1 m2 f2 m3 f3"},
}


def rank_program(g, core, T, topo):
    rank = T.rank_of(core)
    if rank is None:
        return
    A = AluOpType
    AF = ActivationFunctionType
    eng = {"v": g.vector, "a": g.scalar, "p": g.tensor, "g": g, "s": g.sync}
    csem = {"v": "cv", "a": "ca", "p": "cp", "g": "cg"}
    count = {n: 0 for n in SEMAPHORES}
    waited = {n: 0 for n in SEMAPHORES}
    known = {q: {} for q in eng}
    snap = {}
    hist = {}

    def wait(q, sem, val):
        if known[q].get(sem, 0) >= val:
            return
        eng[q].wait_ge(T.sem[sem], val)
        waited[sem] = max(waited[sem], val)
        known[q][sem] = val
        for s2, v2 in snap.get((sem, val), {}).items():
            if known[q].get(s2, 0) < v2:
                known[q][s2] = v2

    def deps(q, reads, writes):
        need = {}
        for acc, is_w in ((reads, False), (writes, True)):
            for (b, lo, hi) in acc:
                ps = b[0] == "P"
                for (l2, h2, w2, q2, sem, val) in hist.get(b, []):
                    if ps:
                        hit = (q2 != q) or (q != "p" and (w2 or is_w) and l2 < hi and lo < h2)
                    else:
                        hit = (w2 or is_w) and l2 < hi and lo < h2
                    if hit and need.get(sem, 0) < val:
                        need[sem] = val
        for sem in sorted(need, key=lambda s: (s == csem.get(q), s)):
            wait(q, sem, need[sem])

    def note(q, reads, writes, sem, val):
        for acc, is_w in ((reads, False), (writes, True)):
            for (b, lo, hi) in acc:
                hist.setdefault(b, []).append((lo, hi, is_w, q, sem, val))

    def op(q, fn, reads, writes):
        deps(q, reads, writes)
        sem = csem[q]
        fn().then_inc(T.sem[sem], 1)
        count[sem] += 1
        snap[(sem, count[sem])] = dict(known[q])
        note(q, reads, writes, sem, count[sem])

    def dma(q, out, in_, reads, writes, sem, total):
        deps(q, reads, writes)
        eng[q].dma_start(out, in_).then_inc(T.sem[sem], 16)
        count[sem] += 16
        sn = snap.setdefault((sem, total), {})
        for s2, v2 in known[q].items():
            sn[s2] = max(sn.get(s2, 0), v2)
        note("d", reads, writes, sem, total)

    peers = [T.cores[(rank + t) % NR] for t in range(1, NR)]
    far = [p for p in peers if topo.chip(p) != topo.chip(core)]
    near = [p for p in peers if topo.chip(p) == topo.chip(core)]

    def split_engines(me, others):
        res, used = {}, set()
        for grp in ([p for p in others if topo.chip(p) != topo.chip(me)],
                    [p for p in others if topo.chip(p) == topo.chip(me)]):
            if not grp:
                continue
            free = [e for e in topo.engines(me, grp[0]) if e not in used]
            n = 1
            while 2 * n * len(grp) <= len(free):
                n *= 2
            for i, p in enumerate(grp):
                res[p] = free[i * n:(i + 1) * n]
                used.update(res[p])
        return res

    mine = split_engines(core, peers)
    n_in = sum(len(split_engines(p, [c for c in T.cores if c != p])[core]) for p in peers)

    def send(src, dst, sem, to):
        deps("g", [(src, peers.index(p) * S, (peers.index(p) + 1) * S) for p in to], [])
        trs = []
        for p in to:
            t = peers.index(p) + 1
            rid, pid, _se = topo.addr(p)
            lo = E + (NR - 1 - t) * S
            trs.append(RemoteDMATransfer(
                dst_ids=[DstId(rid=rid, pnc=pid)], dma_engine_mask=sum(1 << e for e in mine[p]),
                remote_sem=T.sem[sem], src=T[src][:, (t - 1) * S:t * S], dst=T[dst][:, lo:lo + S]))
            count["sent"] += len(mine[p])
        g.remote_dma_fused(trs, local_sem=T.sem.sent)

    def ind(win, whi, off, lo, n):
        return T[win][:, 0:whi].indirect(T[off][:, lo // 16:(lo + n) // 16])

    def gather(q, out, olo, win, whi, off, lo, n, mode):
        o = T[out][:, olo:olo + n]
        rd = [(win, 0, whi), (off, lo // 16, (lo + n) // 16)]
        wr = [(out, olo, olo + n)]
        src = ind(win, whi, off, lo, n)
        if q == "v":
            if mode == "copy":
                op(q, lambda: g.vector.tensor_copy(o, src), rd, wr)
            elif mode == "quarter":
                op(q, lambda: g.vector.tensor_scalar(o, src, 0.25, None, A.mult), rd, wr)
            else:
                op(q, lambda: g.vector.tensor_scalar(o, src, 0.0, None, A.max), rd, wr)
        else:
            if mode == "copy":
                op(q, lambda: g.scalar.activation(o, src, AF.Identity), rd, wr)
            elif mode == "quarter":
                op(q, lambda: g.scalar.activation(o, src, AF.Identity, scale=0.25), rd, wr)
            else:
                op(q, lambda: g.scalar.activation(o, src, AF.Relu), rd, wr)

    def exchange(out, win, mode, sem):
        for grp in (far, near):
            if not grp:
                continue
            pieces = [peers.index(p) * S + k for p in grp for k in (0, S // 2)]
            half = len(pieces) // 2
            for q, part in (("v", pieces[:half]), ("a", pieces[half:])):
                runs = []
                for lo in part:
                    if runs and runs[-1][1] == lo:
                        runs[-1][1] = lo + S // 2
                    else:
                        runs.append([lo, lo + S // 2])
                for lo, hi in runs:
                    gather(q, out, lo, win, E, "sndu", lo, hi - lo, mode)
            send(out, win, sem, grp)
        count[sem] += n_in
        note("r", [], [(win, E, W)], sem, n_in)

    def ts(out, olo, ohi, in_, ilo, ihi, s1, s2, o0, o1=None, ostep=1, istep=1):
        o = T[out][:, olo:ohi:ostep] if ostep > 1 else T[out][:, olo:ohi]
        i = T[in_][:, ilo:ihi:istep] if istep > 1 else T[in_][:, ilo:ihi]
        if o1 is None:
            op("v", lambda: g.vector.tensor_scalar(o, i, s1, None, o0), [(in_, ilo, ihi)], [(out, olo, ohi)])
        else:
            op("v", lambda: g.vector.tensor_scalar(o, i, s1, s2, o0, o1), [(in_, ilo, ihi)], [(out, olo, ohi)])

    def tt(out, olo, n, a, alo, b, blo, o_, ostep=1):
        ohi = olo + n * ostep - (ostep - 1)
        o = T[out][:, olo:ohi:ostep] if ostep > 1 else T[out][:, olo:ohi]
        op("v", lambda: g.vector.tensor_tensor(o, T[a][:, alo:alo + n], T[b][:, blo:blo + n], o_),
           [(a, alo, alo + n), (b, blo, blo + n)], [(out, olo, ohi)])

    def cp(q, out, olo, in_, ilo, n, func=None):
        o, i = T[out][:, olo:olo + n], T[in_][:, ilo:ilo + n]
        if q == "v":
            if func is None:
                op(q, lambda: g.vector.tensor_copy(o, i), [(in_, ilo, ilo + n)], [(out, olo, olo + n)])
            else:
                op(q, lambda: g.vector.tensor_scalar(o, i, 0.0, None, A.max), [(in_, ilo, ilo + n)], [(out, olo, olo + n)])
        else:
            op(q, lambda: g.scalar.activation(o, i, AF.Identity if func is None else func),
               [(in_, ilo, ilo + n)], [(out, olo, olo + n)])

    def memset(buf, lo, hi):
        op("v", lambda: g.vector.memset(T[buf][:, lo:hi], 0.0), [], [(buf, lo, hi)])

    def wrap(ps, bo, src, lo, k, first):
        for h in range(16):
            a0 = bo + 15 - h
            op("p", lambda h=h, a0=a0: g.tensor.matmul(T[ps][:, 0:128], T.base[0:k, a0:a0 + 128],
                                                      T[src][0:k, lo + h:lo + E:16], first and h == 0, h == 15),
               [("base", bo, bo + 144), (src, lo, lo + E)], [(ps, 0, 128)])

    def mm_x(q):
        op("p", lambda: g.tensor.matmul(T["PA%d" % q][:, :], T.Ibf[:, :], T.XW[:, q * Q:(q + 1) * Q], True, False),
           [("Ibf", 0, 128), ("XW", q * Q, (q + 1) * Q)], [("PA%d" % q, 0, Q)])

    def pe(rnd, c, q):
        n = CFG["pe"][rnd][q]
        if c < n:
            lo = c * E + q * Q
            op("p", lambda: g.tensor.matmul(T["PA%d" % q][:, :], T.I32[:, :], T.TM[:, lo:lo + Q], False, c == n - 1),
               [("I32", 0, 128), ("TM", lo, lo + Q)], [("PA%d" % q, 0, Q)])

    def term(c, q, win, whi, off, other):
        lo = c * E + q * Q
        op("v", lambda: g.vector.tensor_tensor(T.TM[:, lo:lo + Q], ind(win, whi, off, lo, Q),
                                               T[other][:, lo:lo + Q], A.mult),
           [(win, 0, whi), (off, lo // 16, (lo + Q) // 16), (other, lo, lo + Q)], [("TM", lo, lo + Q)])

    def idx(c, step):
        lo, pb = c * 128, "PB%d" % c
        if step == 0:
            cp("v", "zi", lo, pb, 0, 128)
        elif step == 1:
            ts("ai", lo, lo + 128, "zi", lo, lo + 128, 63, None, A.bitwise_and)
        elif step == 2:
            tt(pb, 256, 128, pb, 0, "ai", lo, A.not_equal)
            tt("sq", lo, 128, pb, 128, "ai", lo, A.add)
        elif step == 3:
            tt("sq", lo, 128, pb, 256, "sq", lo, A.mult)
        else:
            ts("offu", lo, lo + 128, "sq", lo, lo + 128, 64.0, None, A.mult)

    def finish(rnd, q, out, lo=0, n=Q):
        pa = "PA%d" % q
        if CFG["pe"][rnd][q] == 4:
            cp("a", out, q * Q + lo, pa, lo, n, AF.Relu)
            return False
        for c in range(CFG["pe"][rnd][q], 3):
            tt(pa, lo, n, pa, lo, "TM", c * E + q * Q + lo, A.add)
        tt(out, q * Q + lo, n, pa, lo, "TM", 3 * E + q * Q + lo, A.add)
        return True

    dma("s", T.raw[:, 0:128], T.dirs[:], [], [("raw", 0, 128)], "l_ds", 32)
    dma("a", T.raw[:, 128:256], T.srcs[:], [], [("raw", 128, 256)], "l_ds", 32)
    dma("s", T.sndr[:], T.snd[:], [], [("sndr", 0, 48)], "l_snd", 16)
    dma("a", T.XW[:, 0:1024], T.x[:, 0:1024], [], [("XW", 0, 1024)], "l_x", 32)
    dma("s", T.XW[:, 1024:E], T.x[:, 1024:E], [], [("XW", 1024, E)], "l_x", 32)
    dma("a", T.raw[:, 256:384], T.dsts[:], [], [("raw", 256, 384)], "l_dd", 16)
    op("g", lambda: g.iota(T.pv[:, :], [[-1, 128]], 0, 1, allow_small_or_imprecise_dtypes=True), [], [("pv", 0, 128)])
    memset("KW", 0, E)
    memset("base", 0, 432)
    memset("TAB", 0, TO)
    ts("I32", 0, 128, "pv", 0, 128, 0.0, None, A.is_equal)
    ts("Ibf", 0, 128, "pv", 0, 128, 0.0, None, A.is_equal)
    ts("tiny", 0, 8, "pv", 0, 128, 1.0, 64.0, A.is_ge, A.mult, istep=16)
    ts("tiny", 8, 16, "pv", 0, 128, 3.0, 64.0, A.is_ge, A.mult, istep=16)
    ts("tiny", 16, 24, "pv", 0, 128, 0.0, None, A.is_equal, istep=16)
    cp("v", "cmp", 0, "raw", 0, 256)
    tt("cmp", 384, 128, "raw", 128, "cmp", 128, A.subtract)
    dma("s", T.KW[0:128:16, 0:E], T.cmp[:, 0:128], [("cmp", 0, 128), ("KW", 0, E)], [], "l_kw", 48)
    dma("s", T.KW[1:128:16, 0:E], T.cmp[:, 128:256], [("cmp", 128, 256)], [], "l_kw", 48)
    dma("a", T.KW[2:128:16, 0:E], T.cmp[:, 384:512], [("cmp", 384, 512), ("KW", 0, E)], [], "l_kw", 48)
    note("d", [], [("KW", 0, E)], "l_kw", 48)
    dma("s", T.nbr[:], T.nb[:], [], [("nbr", 0, 512)], "l_nb", 16)
    cp("v", "sndu", 0, "sndr", 0, 48)
    cp("v", "cmp", 256, "raw", 256, 128)
    tt("cmp", 512, 128, "raw", 256, "cmp", 256, A.subtract)
    dma("s", T.DR[0:8, :], T.cmp[:, 256:384], [("cmp", 256, 384)], [], "l_dr", 32)
    dma("s", T.DR[8:16, :], T.cmp[:, 512:640], [("cmp", 512, 640)], [], "l_dr", 32)
    note("d", [], [("DR", 0, E)], "l_dr", 32)
    exchange("SX", "XW", "copy", "arrX")
    tt("tiny", 0, 8, "tiny", 0, "tiny", 8, A.subtract)
    ts("base", 144 + 15, 144 + 143, "pv", 0, 128, 0.0, 1.0 / 64, A.is_equal, A.mult, ostep=16, istep=16)
    ts("tiny", 24, 32, "pv", 0, 8, 0.0, -64.0, A.is_equal, A.mult)
    ts("tiny", 32, 40, "pv", 0, 8, 8.0, -64.0, A.is_equal, A.mult)
    tt("base", 15, 8, "tiny", 0, "tiny", 16, A.add, ostep=16)
    tt("base", 288 + 15, 8, "tiny", 24, "tiny", 32, A.add, ostep=16)
    exchange("SK", "KW", "copy", "arrK")
    wait("s", "sent", count["sent"])
    dma("s", T.TAB[:, TO:TO + 4096], T.tab[:], [], [("TAB", TO, TO + 4096)], "l_tab", 16)
    cp("v", "nbu", 0, "nbr", 0, 512)
    wrap("PA0", 144, "KW", 0, 128, True)
    wrap("PA1", 288, "DR", 0, 16, True)
    for c in range(4):
        ts("PB%d" % c, 128, 256, "PA0", 0, 128, TO / 64.0, None, A.add)
    cp("v", "ND", 0, "PA1", 0, 128)
    for c in range(4):
        op("p", lambda c=c: g.tensor.matmul(T["PB%d" % c][:, 0:128], T.I32[:, :], T.ND[:, :], True, False),
           [("I32", 0, 128), ("ND", 0, 128)], [("PB%d" % c, 0, 128)])
    for q in range(4):
        mm_x(q)

    for q, lst in (("v", CFG["v_list"]), ("a", CFG["a_list"])):
        for it in lst.split():
            lo = int(it[1]) * E + int(it[2]) * Q
            if it[0] == "k":
                gather(q, "G", lo, "KW", W, "nbu", lo, Q, "copy")
            else:
                gather(q, "XG", lo, "XW", W, "nbu", lo, Q, "quarter")
    turned = []

    def turn(k):
        if k not in turned:
            wrap("PB%d" % k, 0, "G", k * E, 128, False)
            turned.append(k)

    turn(0)
    for s in range(5):
        idx(0, s)
    todo = []
    for c in range(4):
        for q in range(4):
            if c < 3 and q >= CFG["ipos"][c]:
                turn(c + 1)
                idx(c + 1, q - CFG["ipos"][c])
            term(c, q, "TAB", TO + 4096, "offu", "XG")
            if (c, q) in CFG["wpos"]:
                turn(CFG["wpos"].index((c, q)) + 1)
            pe(1, c, q)
            if c == 3 and q > 0:
                if finish(1, q - 1, "MW1"):
                    cp("a", "MW1", (q - 1) * Q, "MW1", (q - 1) * Q, Q, AF.Relu)
        if c < 3:
            for s in range(4 - CFG["ipos"][c], 5):
                idx(c + 1, s)
    if finish(1, 3, "MW1"):
        todo.append(3)

    for rnd, win, sbuf, sem, out in ((2, "MW1", "SM1", "arr1", "MW2"), (3, "MW2", "SM2", "arr2", "YB")):
        exchange(sbuf, win, "relu", sem)
        for q in todo:
            cp("v", win, q * Q, win, q * Q, Q, AF.Relu)
        todo = []
        for q in range(4):
            mm_x(q)
        if rnd == 2:
            order = [(c, q) for q in range(4) for c in range(3)]
            for i, (c, q) in enumerate(order):
                lo = c * E + q * Q
                gather("v" if i < CFG["w_v"] else "a", "WT", lo, "TAB", TO + 4096, "offu", lo, Q, "quarter")
            for q in range(4):
                gather("a", "WT", 3 * E + q * Q, "TAB", TO + 4096, "offu", 3 * E + q * Q, Q, "quarter")
            for q in range(4):
                cp("a", "PB%d" % q, 0, "WT", 3 * E + q * Q, Q)
        for q in range(4):
            gather("a", "XG", 3 * E + q * Q, win, W, "nbu", 3 * E + q * Q, Q, "copy")
        for it in CFG["order"][rnd].split():
            q = int(it[1])
            if it[0] == "t":
                for c in range(3):
                    term(c, q, win, W, "nbu", "WT")
                    pe(rnd, c, q)
            elif it[0] == "m":
                tt("TM", 3 * E + q * Q, Q, "XG", 3 * E + q * Q, "PB%d" % q, 0, A.mult)
                pe(rnd, 3, q)
            elif rnd == 2:
                if finish(rnd, q, out):
                    if q < 3:
                        cp("a", out, q * Q, out, q * Q, Q, AF.Relu)
                    else:
                        todo.append(q)
            else:
                for lo, n in ([(0, Q)] if q < 3 else [(0, Q // 2), (Q // 2, Q // 2)]):
                    a0 = q * Q + lo
                    if finish(rnd, q, out, lo, n):
                        cp("a", out, a0, out, a0, n, AF.Relu)
                    dma("s", T.y[:, a0:a0 + n], T.YB[:, a0:a0 + n], [("YB", a0, a0 + n)], [], "st", 80)

    wait("s", "st", 80)
    for sem in SEMAPHORES:
        if waited[sem] < count[sem]:
            known["g"][sem] = 0
            wait("g", sem, count[sem])
